import numpy as np
import ml_dtypes


def mxq(x, axis, fmt="e4m3"):
    dtype, down = {"e4m3": (ml_dtypes.float8_e4m3fn, 7), "e5m2": (ml_dtypes.float8_e5m2, 14)}[fmt]
    v = np.moveaxis(np.asarray(x, np.float32).astype(ml_dtypes.bfloat16).astype(np.float64), axis, -1)
    blocks = v.reshape(v.shape[:-1] + (-1, 32))
    amax = np.abs(blocks).max(-1, keepdims=True)
    byte = np.maximum(np.where(amax > 0, np.frexp(amax)[1] - 1 + 127, 0) - down, 1)
    scale = np.exp2(byte - 127.0)
    codes = (blocks / scale).astype(np.float32).astype(dtype).astype(np.float64)
    return np.moveaxis((codes * scale).reshape(v.shape), -1, axis)


WIDE = False


def mx_kscale(k):
    if not WIDE:
        return np.ones(k)
    levels = np.array([10, -10, 5, -5, 0])
    if k % 512:
        return np.exp2(np.random.permutation(np.resize(levels, k // 32))).repeat(32)
    a = np.empty((k // 512, 16))
    for p in range(k // 512):
        a[p, :8] = np.random.permutation(np.resize(levels, 8))
        for g in range(8):
            far = levels[np.abs(levels - a[p, g]) >= 10]
            a[p, g + 8] = far[np.random.randint(len(far))]
    return np.exp2(a.ravel()).repeat(32)


def f64(x):
    return np.asarray(x).astype(np.float64)


def striped(idx):
    return np.tile(idx.reshape(-1, 16).T, (8, 1)).astype(np.uint16)


def unstriped(offs):
    return offs[:16].T.reshape(-1).astype(np.int64)


def pack_weight(w):
    k, n = w.shape
    w = f64(np.asarray(w, np.float32).astype(ml_dtypes.bfloat16)).reshape(k // 32, 32, n)
    amax = np.abs(w).max(1)
    byte = np.clip(np.where(amax > 0, np.frexp(amax)[1] - 1 + 127 - 7, 1), 1, 254)
    scaled = (w * np.exp2(127.0 - byte)[:, None, :]).reshape(k, n).astype(np.float32)
    words = np.ascontiguousarray(scaled.reshape(k // 512, 128, 4, n).transpose(0, 1, 3, 2)).astype(ml_dtypes.float8_e4m3fn).view(np.uint8)
    return words, np.ascontiguousarray(byte.astype(np.uint8).reshape(k // 512, 16, n))


def unpack_weight(words, scales):
    g, p, n, _ = words.shape
    vals = np.ascontiguousarray(words).view(ml_dtypes.float8_e4m3fn).astype(np.float64) * np.repeat(np.exp2(scales.astype(np.float64) - 127.0), 8, axis=1)[..., None]
    return vals.transpose(0, 1, 3, 2).reshape(g * 512, n)


def sigmoid(v):
    return 1.0 / (1.0 + np.exp(-np.maximum(v, -700.0)))


K, T, S, V, N, D = 1024, 1024, 512, 256, 128, 3
P = 2 ** 7


def setup_inputs():
    n = np.random.standard_normal
    s = mx_kscale(K)[:, None]
    near = np.random.permutation(S)
    packed_xT = pack_weight(n((K, T)) * s)
    return {
        "x_words": packed_xT[0],
        "x_scales": packed_xT[1],
        "w1": (n((K, N)) / np.sqrt(K) / s).astype(np.float32),
        "w2": (n((K, N)) / np.sqrt(K) / s).astype(np.float32),
        "w3": (n((K, N)) / np.sqrt(K) / s).astype(np.float32),
        "pos": (np.tile(n((D, 1, V)) * 0.7, (1, P, 1))).astype(np.float32),
        "offs": striped(np.random.permutation(T)[:S]),
        "pos1": striped(near[:V]),
        "pos2": striped(near[V:]),
        "pos3": striped(np.random.permutation(S)[:V]),
        "own": striped(np.random.permutation(S)[:V]),
    }


def reference(x_words, x_scales, w1, w2, w3, pos, offs, pos1, pos2, pos3, own):
    xq = unpack_weight(x_words, x_scales)[:, unstriped(offs)]
    rr = sigmoid(mxq(f64(w3), 0, "e4m3").T @ xq)
    vv = mxq(f64(w2), 0, "e4m3").T @ xq
    kk = mxq(f64(w1), 0, "e4m3").T @ xq
    e0 = np.exp(kk[:, unstriped(pos1)] + f64(pos)[0, :1])
    e1 = np.exp(kk[:, unstriped(pos2)] + f64(pos)[1, :1])
    e2 = np.exp(kk[:, unstriped(pos3)] + f64(pos)[2, :1])
    num = vv[:, unstriped(pos1)] * e0 + vv[:, unstriped(pos2)] * e1 + vv[:, unstriped(pos3)] * e2
    den = e0 + e1 + e2
    return rr[:, unstriped(own)] * (num / den)

@@ -1,0 +1,155 @@
+from contextlib import ExitStack
+
+import concourse.mybir as mybir
+
+K, T, S, V, N, D = 1024, 1024, 512, 256, 128, 3
+FLOPS = 2 * 3 * K * N * S
+
+F32 = mybir.dt.float32
+BF16 = mybir.dt.bfloat16
+I32 = mybir.dt.int32
+U32 = mybir.dt.uint32
+U16 = mybir.dt.uint16
+U8 = mybir.dt.uint8
+FP8X4 = mybir.dt.float8_e4m3fn_x4
+ALU = mybir.AluOpType
+ACT = mybir.ActivationFunctionType
+
+P = 128
+PACK = 4
+PASSES = K // (P * PACK)
+HALF = S // 2
+
+
+def tile_picked_yaft_aft_p_kernel(tc, x_words, x_scales, w1, w2, w3, pos, offs, pos1, pos2, pos3, own, out):
+    nc = tc.nc
+    with ExitStack() as ctx:
+        lists = ctx.enter_context(tc.tile_pool(name="lists", bufs=1))
+        sb = ctx.enter_context(tc.tile_pool(name="sb", bufs=1))
+        psum = ctx.enter_context(tc.psum_pool(name="psum", bufs=1))
+
+        def load_list(src, name):
+            tile = lists.tile([P, src.shape[1]], U16, name=name)
+            nc.sync.dma_start(tile[:], src)
+            return tile
+
+        def load_words(g):
+            tile = sb.tile([P, T], U32, name="x_words_%d" % g, align_bytes=64)
+            nc.sync.dma_start(tile[:].bitcast(I32), x_words[g].rearrange("p n t -> p (n t)").bitcast(I32))
+            return tile
+
+        def load_weight(w, name):
+            tile = sb.tile([P, PASSES, PACK * N], F32, name=name + "_raw", align_bytes=64)
+            nc.sync.dma_start(tile[:], w.rearrange("(g p t) m -> p g (t m)", g=PASSES, t=PACK))
+            return tile
+
+        def round_weight(raw, name):
+            tile = sb.tile([P, PASSES * N * PACK], BF16, name=name + "_bf16", align_bytes=64)
+            nc.scalar.copy(tile[:].rearrange("p (g m t) -> p g m t", g=PASSES, t=PACK),
+                           raw[:].rearrange("p g (t m) -> p g m t", t=PACK))
+            return tile
+
+        def quantize_weight(rounded, name):
+            codes = sb.tile([P, PASSES * N], U32, name=name + "_codes", align_bytes=64)
+            scales = sb.tile([P, PASSES * N], U8, name=name + "_scales", align_bytes=64)
+            nc.vector.quantize_mx(out=codes[:].bitcast(FP8X4), scales=scales[:], in_=rounded[:])
+            return codes, scales
+
+        def product_pass(acc, weight, g, cols):
+            codes, scales = weight
+            nc.tensor.matmul_mx(
+                out=acc[:],
+                lhsT=codes[:, g * N : (g + 1) * N].bitcast(FP8X4),
+                lhsT_scale=scales[:, g * N : (g + 1) * N],
+                rhs=picked_words[g][:, cols].bitcast(FP8X4),
+                rhs_scale=picked_scales[PACK * g : P, cols],
+                start=(g == 0),
+                stop=(g == PASSES - 1),
+            )
+
+        def values(name):
+            return sb.tile([P, V], F32, name=name, align_bytes=64)
+
+        x_planes = sb.tile([P, T], U8, name="x_planes", align_bytes=64)
+        nc.vector.memset(x_planes[:].bitcast(I32), 0)
+
+        offs_t = load_list(offs, "offs_t")
+        words0 = load_words(0)
+        for q in range(4):
+            nc.sync.dma_start(x_planes[32 * q : 32 * q + 4 * PASSES, :].bitcast(I32),
+                              x_scales[:, 4 * q : 4 * q + 4, :].bitcast(I32))
+        w1_raw = load_weight(w1, "w1")
+        words1 = load_words(1)
+        bias = sb.tile([P, D, V], F32, name="bias", align_bytes=64)
+        nc.sync.dma_start(bias[:], pos.rearrange("d p v -> p d v"))
+        w2_raw = load_weight(w2, "w2")
+        p0 = load_list(pos1, "p0")
+        p1 = load_list(pos2, "p1")
+        p2 = load_list(pos3, "p2")
+        own_t = load_list(own, "own_t")
+        w3_raw = load_weight(w3, "w3")
+
+        picked_words = [sb.tile([P, S], U32, name="picked_words_%d" % g, align_bytes=64) for g in range(PASSES)]
+        picked_scales = sb.tile([P, S], U8, name="picked_scales", align_bytes=64)
+        halves = [slice(h * HALF, (h + 1) * HALF) for h in range(2)]
+        offs_halves = [offs_t[:, h * HALF // 16 : (h + 1) * HALF // 16] for h in range(2)]
+
+        w1_bf = round_weight(w1_raw, "w1")
+        nc.vector.tensor_copy(picked_words[0][:], words0[:].indirect(offs_t[:]))
+        nc.vector.tensor_copy(picked_scales[:], x_planes[:].indirect(offs_t[:]))
+        nc.vector.tensor_copy(picked_words[1][:, halves[0]], words1[:].indirect(offs_halves[0]))
+        w1_q = quantize_weight(w1_bf, "w1")
+        nc.vector.tensor_copy(picked_words[1][:, halves[1]], words1[:].indirect(offs_halves[1]))
+
+        kk = sb.tile([P, S], F32, name="kk", align_bytes=64)
+        for h in range(2):
+            acc = psum.tile([P, HALF], F32, name="kk_acc_%d" % h)
+            for g in range(PASSES):
+                product_pass(acc, w1_q, g, halves[h])
+            nc.scalar.copy(kk[:, halves[h]], acc[:])
+
+        w2_bf = round_weight(w2_raw, "w2")
+        w3_bf = round_weight(w3_raw, "w3")
+
+        a0, a1, a2 = values("a0"), values("a1"), values("a2")
+        nc.vector.tensor_tensor(a1[:], kk[:].indirect(p1[:]), bias[:, 1, :], ALU.add)
+        w2_q = quantize_weight(w2_bf, "w2")
+        vv_acc = psum.tile([P, S], F32, name="vv_acc")
+        for g in range(PASSES):
+            product_pass(vv_acc, w2_q, g, slice(0, S))
+        vv = sb.tile([P, S], F32, name="vv", align_bytes=64)
+        nc.scalar.copy(vv[:], vv_acc[:])
+        nc.vector.tensor_tensor(a2[:], kk[:].indirect(p2[:]), bias[:, 2, :], ALU.add)
+        w3_q = quantize_weight(w3_bf, "w3")
+        gate_acc = psum.tile([P, S], F32, name="gate_acc")
+        for g in range(PASSES):
+            product_pass(gate_acc, w3_q, g, slice(0, S))
+        gate_tanh = sb.tile([P, S], F32, name="gate_tanh", align_bytes=64)
+        nc.scalar.activation(gate_tanh[:], gate_acc[:], ACT.Tanh, scale=0.5)
+        nc.vector.tensor_tensor(a0[:], kk[:].indirect(p0[:]), bias[:, 0, :], ALU.add)
+
+        d12, d01, d02 = values("d12"), values("d01"), values("d02")
+        e12, t01, e02 = values("e12"), values("t01"), values("e02")
+        nc.vector.tensor_tensor(d12[:], a1[:], a2[:], ALU.subtract)
+        nc.scalar.activation(e12[:], d12[:], ACT.Exp)
+        nc.vector.tensor_tensor(d01[:], a0[:], a1[:], ALU.subtract)
+        nc.scalar.activation(t01[:], d01[:], ACT.Tanh, scale=0.5)
+        nc.vector.tensor_tensor(d02[:], a0[:], a2[:], ALU.subtract)
+        nc.scalar.activation(e02[:], d02[:], ACT.Exp)
+
+        v1, dv, den, root, half_w2 = values("v1"), values("dv"), values("den"), values("root"), values("half_w2")
+        nc.vector.tensor_copy(v1[:], vv[:].indirect(p1[:]))
+        nc.vector.scalar_tensor_tensor(den[:], e02[:], 1.0, e12[:], ALU.add, ALU.add)
+        nc.scalar.activation(root[:], den[:], ACT.Abs_reciprocal_sqrt, scale=2.0)
+        nc.scalar.activation(half_w2[:], root[:], ACT.Square)
+        nc.vector.tensor_tensor(dv[:], vv[:].indirect(p0[:]), v1[:], ALU.subtract)
+        own_tanh = values("own_tanh")
+        nc.vector.tensor_copy(own_tanh[:], gate_tanh[:].indirect(own_t[:]))
+        step, mean, rest, pull, half_mix, result = values("step"), values("mean"), values("rest"), values("pull"), values("half_mix"), values("result")
+        nc.vector.scalar_tensor_tensor(step[:], t01[:], 1.0, dv[:], ALU.add, ALU.mult)
+        nc.vector.scalar_tensor_tensor(mean[:], step[:], 0.5, v1[:], ALU.mult, ALU.add)
+        nc.vector.tensor_tensor(rest[:], vv[:].indirect(p2[:]), mean[:], ALU.subtract)
+        nc.vector.tensor_tensor(pull[:], rest[:], half_w2[:], ALU.mult)
+        nc.vector.scalar_tensor_tensor(half_mix[:], mean[:], 0.5, pull[:], ALU.mult, ALU.add)
+        nc.vector.scalar_tensor_tensor(result[:], own_tanh[:], 1.0, half_mix[:], ALU.add, ALU.mult)
+        nc.sync.dma_start(out, result[:])

@@ -1,6 +1,7 @@
 from contextlib import ExitStack
 
 import concourse.mybir as mybir
+from concourse.masks import make_identity
 
 K, T, S, V, N, D = 1024, 1024, 512, 256, 128, 3
 FLOPS = 2 * 3 * K * N * S
@@ -26,6 +27,7 @@ def tile_picked_yaft_aft_p_kernel(tc, x_words, x_scales, w1, w2, w3, pos, offs, 
     with ExitStack() as ctx:
         lists = ctx.enter_context(tc.tile_pool(name="lists", bufs=1))
         sb = ctx.enter_context(tc.tile_pool(name="sb", bufs=1))
+        reuse = ctx.enter_context(tc.tile_pool(name="reuse", bufs=1))
         psum = ctx.enter_context(tc.psum_pool(name="psum", bufs=1))
 
         def load_list(src, name):
@@ -38,29 +40,26 @@ def tile_picked_yaft_aft_p_kernel(tc, x_words, x_scales, w1, w2, w3, pos, offs, 
             nc.sync.dma_start(tile[:].bitcast(I32), x_words[g].rearrange("p n t -> p (n t)").bitcast(I32))
             return tile
 
-        def load_weight(w, name):
-            tile = sb.tile([P, PASSES, PACK * N], F32, name=name + "_raw", align_bytes=64)
-            nc.sync.dma_start(tile[:], w.rearrange("(g p t) m -> p g (t m)", g=PASSES, t=PACK))
-            return tile
+        def load_weight(tile, w, g):
+            rows = w.rearrange("(g p t) m -> g p (t m)", g=PASSES, t=PACK)
+            nc.sync.dma_start(tile, rows[g])
 
-        def round_weight(raw, name):
-            tile = sb.tile([P, PASSES * N * PACK], BF16, name=name + "_bf16", align_bytes=64)
-            nc.scalar.copy(tile[:].rearrange("p (g m t) -> p g m t", g=PASSES, t=PACK),
-                           raw[:].rearrange("p g (t m) -> p g m t", t=PACK))
-            return tile
+        def round_pass(copy, rounded, raw):
+            copy(rounded.rearrange("p (c i t) -> p c t i", i=4, t=PACK), raw.rearrange("p (t c i) -> p c t i", t=PACK, i=4))
 
-        def quantize_weight(rounded, name):
-            codes = sb.tile([P, PASSES * N], U32, name=name + "_codes", align_bytes=64)
-            scales = sb.tile([P, PASSES * N], U8, name=name + "_scales", align_bytes=64)
+        def quantize_weight(rounded, name, tag=""):
+            width = rounded.shape[1] // PACK
+            codes = sb.tile([P, width], U32, name=name + "_codes", tag=tag, align_bytes=64)
+            scales = sb.tile([P, width], U8, name=name + "_scales", align_bytes=64)
             nc.vector.quantize_mx(out=codes[:].bitcast(FP8X4), scales=scales[:], in_=rounded[:])
-            return codes, scales
+            return [(codes[:, c : c + N], scales[:, c : c + N]) for c in range(0, width, N)]
 
         def product_pass(acc, weight, g, cols):
-            codes, scales = weight
+            codes, scales = weight[g]
             nc.tensor.matmul_mx(
                 out=acc[:],
-                lhsT=codes[:, g * N : (g + 1) * N].bitcast(FP8X4),
-                lhsT_scale=scales[:, g * N : (g + 1) * N],
+                lhsT=codes.bitcast(FP8X4),
+                lhsT_scale=scales,
                 rhs=picked_words[g][:, cols].bitcast(FP8X4),
                 rhs_scale=picked_scales[PACK * g : P, cols],
                 start=(g == 0),
@@ -78,78 +77,135 @@ def tile_picked_yaft_aft_p_kernel(tc, x_words, x_scales, w1, w2, w3, pos, offs, 
         for q in range(4):
             nc.sync.dma_start(x_planes[32 * q : 32 * q + 4 * PASSES, :].bitcast(I32),
                               x_scales[:, 4 * q : 4 * q + 4, :].bitcast(I32))
-        w1_raw = load_weight(w1, "w1")
+        def raw_pass(name):
+            return sb.tile([P, PACK * N], F32, name=name, tag=name, align_bytes=64)
+
+        w1_raw = [raw_pass("w1_raw_%d" % g) for g in range(PASSES)]
+        for g in range(PASSES):
+            load_weight(w1_raw[g][:], w1, g)
         words1 = load_words(1)
-        bias = sb.tile([P, D, V], F32, name="bias", align_bytes=64)
-        nc.sync.dma_start(bias[:], pos.rearrange("d p v -> p d v"))
-        w2_raw = load_weight(w2, "w2")
-        p0 = load_list(pos1, "p0")
+        w2_raw = [raw_pass("w2_raw_%d" % g) for g in range(PASSES)]
+        for g in range(PASSES):
+            load_weight(w2_raw[g][:], w2, g)
         p1 = load_list(pos2, "p1")
         p2 = load_list(pos3, "p2")
+        p0 = load_list(pos1, "p0")
+        w3_raw = reuse.tile([P, PASSES, PACK * N], F32, name="w3_raw", offset=0, align_bytes=64)
+        for g in range(PASSES):
+            load_weight(w3_raw[:, g, :], w3, g)
+        bias = sb.tile([P, D, 2], F32, name="bias", align_bytes=64)
+        with nc.allow_non_contiguous_dma(reason="one bias value a partition"):
+            nc.sync.dma_start(bias[:].rearrange("v d c -> v (d c)"),
+                              pos.rearrange("d p (c v) -> (d p c) v", c=2)[0 : D * P * 2 : P + 1, :].rearrange("j v -> v j"))
         own_t = load_list(own, "own_t")
-        w3_raw = load_weight(w3, "w3")
 
-        picked_words = [sb.tile([P, S], U32, name="picked_words_%d" % g, align_bytes=64) for g in range(PASSES)]
+        identity = sb.tile([P, P], F32, name="identity", align_bytes=64)
+        make_identity(nc, identity[:])
+
         picked_scales = sb.tile([P, S], U8, name="picked_scales", align_bytes=64)
+        picked_words = [sb.tile([P, S], U32, name="picked_words_0", align_bytes=64)]
         halves = [slice(h * HALF, (h + 1) * HALF) for h in range(2)]
-        offs_halves = [offs_t[:, h * HALF // 16 : (h + 1) * HALF // 16] for h in range(2)]
+        parts = [slice(c * P, (c + 1) * P) for c in range(2)]
 
-        w1_bf = round_weight(w1_raw, "w1")
+        w1_bf = [sb.tile([P, PACK * N], BF16, name="w1_bf16_%d" % g, align_bytes=64) for g in range(PASSES)]
+        for g in range(PASSES):
+            round_pass(nc.scalar.copy, w1_bf[g][:], w1_raw[g][:])
         nc.vector.tensor_copy(picked_words[0][:], words0[:].indirect(offs_t[:]))
         nc.vector.tensor_copy(picked_scales[:], x_planes[:].indirect(offs_t[:]))
-        nc.vector.tensor_copy(picked_words[1][:, halves[0]], words1[:].indirect(offs_halves[0]))
-        w1_q = quantize_weight(w1_bf, "w1")
-        nc.vector.tensor_copy(picked_words[1][:, halves[1]], words1[:].indirect(offs_halves[1]))
-
-        kk = sb.tile([P, S], F32, name="kk", align_bytes=64)
+        w1_q = quantize_weight(w1_bf[0], "w1a") + quantize_weight(w1_bf[1], "w1b", "w1b_codes")
+        picked_words.append(sb.tile([P, S], U32, name="picked_words_1", tag="w1_raw_1", align_bytes=64))
         for h in range(2):
-            acc = psum.tile([P, HALF], F32, name="kk_acc_%d" % h)
-            for g in range(PASSES):
-                product_pass(acc, w1_q, g, halves[h])
-            nc.scalar.copy(kk[:, halves[h]], acc[:])
-
-        w2_bf = round_weight(w2_raw, "w2")
-        w3_bf = round_weight(w3_raw, "w3")
-
-        a0, a1, a2 = values("a0"), values("a1"), values("a2")
-        nc.vector.tensor_tensor(a1[:], kk[:].indirect(p1[:]), bias[:, 1, :], ALU.add)
+            nc.vector.tensor_copy(picked_words[1][:, halves[h]], words1[:].indirect(offs_t[:, h * HALF // 16 : (h + 1) * HALF // 16]))
+        w2_bf = sb.tile([P, PASSES * PACK * N], BF16, name="w2_bf16", tag="w2_bf16", align_bytes=64)
+        round_pass(nc.scalar.copy, w2_bf[:, : PACK * N], w2_raw[0][:])
+        round_pass(nc.vector.tensor_copy, w2_bf[:, PACK * N :], w2_raw[1][:])
         w2_q = quantize_weight(w2_bf, "w2")
-        vv_acc = psum.tile([P, S], F32, name="vv_acc")
+
+        kk = sb.tile([P, S], F32, name="kk", tag="w2_raw_0", align_bytes=64)
+        kk_acc = [psum.tile([P, HALF], F32, name="kk_acc_%d" % h, tag="kk_acc_%d" % h) for h in range(2)]
+        for g in range(PASSES):
+            for h in range(2):
+                product_pass(kk_acc[h], w1_q, g, halves[h])
+        for h in range(2):
+            nc.scalar.copy(kk[:, halves[h]], kk_acc[h][:])
+        vv_acc = psum.tile([P, S], F32, name="vv_acc", tag="vv_acc")
         for g in range(PASSES):
             product_pass(vv_acc, w2_q, g, slice(0, S))
-        vv = sb.tile([P, S], F32, name="vv", align_bytes=64)
-        nc.scalar.copy(vv[:], vv_acc[:])
-        nc.vector.tensor_tensor(a2[:], kk[:].indirect(p2[:]), bias[:, 2, :], ALU.add)
-        w3_q = quantize_weight(w3_bf, "w3")
-        gate_acc = psum.tile([P, S], F32, name="gate_acc")
+
+        w3_bf = sb.tile([P, PASSES * PACK * N], BF16, name="w3_bf16", tag="w1b_codes", align_bytes=64)
+        for g in range(PASSES):
+            round_pass(nc.scalar.copy, w3_bf[:, g * PACK * N : (g + 1) * PACK * N], w3_raw[:, g, :])
+
+        k1 = sb.tile([P, V], F32, name="k1", tag="w2_bf16", align_bytes=64)
+        k2 = values("k2")
+        nc.vector.tensor_copy(k1[:], kk[:].indirect(p1[:]))
+        nc.vector.tensor_copy(k2[:], kk[:].indirect(p2[:]))
+        w3_q = quantize_weight(w3_bf, "w3", "w3_codes")
+        gate_acc = psum.tile([P, S], F32, name="gate_acc", tag="gate_acc")
         for g in range(PASSES):
             product_pass(gate_acc, w3_q, g, slice(0, S))
+        vv = reuse.tile([P, S], F32, name="vv", offset=0, align_bytes=64)
+        nc.scalar.copy(vv[:], vv_acc[:])
         gate_tanh = sb.tile([P, S], F32, name="gate_tanh", align_bytes=64)
         nc.scalar.activation(gate_tanh[:], gate_acc[:], ACT.Tanh, scale=0.5)
-        nc.vector.tensor_tensor(a0[:], kk[:].indirect(p0[:]), bias[:, 0, :], ALU.add)
 
-        d12, d01, d02 = values("d12"), values("d01"), values("d02")
-        e12, t01, e02 = values("e12"), values("t01"), values("e02")
-        nc.vector.tensor_tensor(d12[:], a1[:], a2[:], ALU.subtract)
-        nc.scalar.activation(e12[:], d12[:], ACT.Exp)
-        nc.vector.tensor_tensor(d01[:], a0[:], a1[:], ALU.subtract)
-        nc.scalar.activation(t01[:], d01[:], ACT.Tanh, scale=0.5)
-        nc.vector.tensor_tensor(d02[:], a0[:], a2[:], ALU.subtract)
-        nc.scalar.activation(e02[:], d02[:], ACT.Exp)
+        k12 = reuse.tile([P, V], F32, name="k12", offset=2048, align_bytes=64)
+        gaps = reuse.tile([P, 2, 2, 2], F32, name="gaps", offset=3072, align_bytes=64)
+        k01 = reuse.tile([P, V], F32, name="k01", offset=3136, align_bytes=64)
+        half_gap01 = sb.tile([P, 2], F32, name="half_gap01", align_bytes=64)
+        nc.vector.tensor_tensor(gaps[:], bias[:, 0:2, :].unsqueeze(2).to_broadcast([P, 2, 2, 2]),
+                                bias[:, 1:3, :].unsqueeze(1).to_broadcast([P, 2, 2, 2]), ALU.subtract)
+        nc.vector.tensor_tensor(k12[:], k1[:], k2[:], ALU.subtract)
+        nc.vector.tensor_scalar(half_gap01[:], gaps[:, 0, 0, :], 0.5, None, ALU.mult)
+        for c in range(2):
+            nc.vector.tensor_tensor(k01[:, parts[c]], kk[:].indirect(p0[:, c * P // 16 : (c + 1) * P // 16]), k1[:, parts[c]], ALU.subtract)
 
-        v1, dv, den, root, half_w2 = values("v1"), values("dv"), values("den"), values("root"), values("half_w2")
-        nc.vector.tensor_copy(v1[:], vv[:].indirect(p1[:]))
-        nc.vector.scalar_tensor_tensor(den[:], e02[:], 1.0, e12[:], ALU.add, ALU.add)
-        nc.scalar.activation(root[:], den[:], ACT.Abs_reciprocal_sqrt, scale=2.0)
-        nc.scalar.activation(half_w2[:], root[:], ACT.Square)
-        nc.vector.tensor_tensor(dv[:], vv[:].indirect(p0[:]), v1[:], ALU.subtract)
-        own_tanh = values("own_tanh")
-        nc.vector.tensor_copy(own_tanh[:], gate_tanh[:].indirect(own_t[:]))
+        def turn(acc, src, start, stop):
+            nc.tensor.matmul(acc, src, identity[:], start=start, stop=stop, is_transpose=True)
+
+        k12_t = psum.tile([P, V], F32, name="k12_t")
+        k01_t = [psum.tile([P, P], F32, name="k01_t_%d" % c) for c in range(2)]
+        k02_t = [psum.tile([P, P], F32, name="k02_t_%d" % c, tag="kk_acc_%d" % c) for c in range(2)]
+        e12_t, e02_t, t01_t = values("e12_t"), values("e02_t"), values("t01_t")
+        for c in range(2):
+            turn(k12_t[:, parts[c]], k12[:, parts[c]], True, True)
+        for c in range(2):
+            turn(k02_t[c][:], k12[:, parts[c]], True, False)
+        for c in range(2):
+            nc.scalar.activation(e12_t[:, parts[c]], k12_t[:, parts[c]], ACT.Exp, bias=gaps[:, 1, 1, c : c + 1])
+        for c in range(2):
+            turn(k01_t[c][:], k01[:, parts[c]], True, True)
+            turn(k02_t[c][:], k01[:, parts[c]], False, True)
+            nc.scalar.activation(t01_t[:, parts[c]], k01_t[c][:], ACT.Tanh, bias=half_gap01[:, c : c + 1], scale=0.5)
+            nc.scalar.activation(e02_t[:, parts[c]], k02_t[c][:], ACT.Exp, bias=gaps[:, 0, 1, c : c + 1])
+        t01 = psum.tile([P, V], F32, name="t01", tag="vv_acc")
+        for c in range(2):
+            turn(t01[:, parts[c]], t01_t[:, parts[c]], True, True)
+        e_sum = psum.tile([P, V], F32, name="e_sum", tag="gate_acc")
+        root, half_w2 = values("root"), values("half_w2")
+        for c in parts:
+            turn(e_sum[:, c], e12_t[:, c], True, False)
+            turn(e_sum[:, c], e02_t[:, c], False, True)
+        for c in parts:
+            nc.scalar.activation(root[:, c], e_sum[:, c], ACT.Abs_reciprocal_sqrt, bias=2.0, scale=2.0)
+        for c in parts:
+            nc.scalar.activation(half_w2[:, c], root[:, c], ACT.Square)
+
+        v1, dv, own_tanh = values("v1"), values("dv"), values("own_tanh")
         step, mean, rest, pull, half_mix, result = values("step"), values("mean"), values("rest"), values("pull"), values("half_mix"), values("result")
-        nc.vector.scalar_tensor_tensor(step[:], t01[:], 1.0, dv[:], ALU.add, ALU.mult)
-        nc.vector.scalar_tensor_tensor(mean[:], step[:], 0.5, v1[:], ALU.mult, ALU.add)
-        nc.vector.tensor_tensor(rest[:], vv[:].indirect(p2[:]), mean[:], ALU.subtract)
-        nc.vector.tensor_tensor(pull[:], rest[:], half_w2[:], ALU.mult)
-        nc.vector.scalar_tensor_tensor(half_mix[:], mean[:], 0.5, pull[:], ALU.mult, ALU.add)
-        nc.vector.scalar_tensor_tensor(result[:], own_tanh[:], 1.0, half_mix[:], ALU.add, ALU.mult)
-        nc.sync.dma_start(out, result[:])
+        nc.vector.tensor_copy(v1[:], vv[:].indirect(p1[:]))
+        nc.vector.tensor_copy(own_tanh[:], gate_tanh[:].indirect(own_t[:]))
+        nc.vector.tensor_tensor(dv[:], vv[:].indirect(p0[:]), v1[:], ALU.subtract)
+        for c in parts:
+            nc.vector.scalar_tensor_tensor(step[:, c], t01[:, c], 1.0, dv[:, c], ALU.add, ALU.mult)
+        for c in parts:
+            nc.vector.scalar_tensor_tensor(mean[:, c], step[:, c], 0.5, v1[:, c], ALU.mult, ALU.add)
+        for h in range(2):
+            nc.vector.tensor_tensor(rest[:, parts[h]], vv[:].indirect(p2[:, h * V // 32 : (h + 1) * V // 32]), mean[:, parts[h]], ALU.subtract)
+        for c in parts:
+            nc.vector.tensor_tensor(pull[:, c], rest[:, c], half_w2[:, c], ALU.mult)
+        for c in parts:
+            nc.vector.scalar_tensor_tensor(half_mix[:, c], mean[:, c], 0.5, pull[:, c], ALU.mult, ALU.add)
+        for c in parts:
+            nc.vector.scalar_tensor_tensor(result[:, c], own_tanh[:, c], 1.0, half_mix[:, c], ALU.add, ALU.mult)
+            nc.sync.dma_start(out[:, c], result[:, c])

@@ -192,7 +192,8 @@ def tile_picked_yaft_aft_p_kernel(tc, x_words, x_scales, w1, w2, w3, pos, offs, 
             nc.scalar.activation(half_w2[:, c], root[:, c], ACT.Square)
 
         v1, dv, own_tanh = values("v1"), values("dv"), values("own_tanh")
-        step, mean, rest, pull, half_mix, result = values("step"), values("mean"), values("rest"), values("pull"), values("half_mix"), values("result")
+        step, mean, rest, pull, result = values("step"), values("mean"), values("rest"), values("pull"), values("result")
+        gated_mean, gated_rest = values("gated_mean"), values("gated_rest")
         nc.vector.tensor_copy(v1[:], vv[:].indirect(p1[:]))
         nc.vector.tensor_copy(own_tanh[:], gate_tanh[:].indirect(own_t[:]))
         nc.vector.tensor_tensor(dv[:], vv[:].indirect(p0[:]), v1[:], ALU.subtract)
@@ -202,10 +203,10 @@ def tile_picked_yaft_aft_p_kernel(tc, x_words, x_scales, w1, w2, w3, pos, offs, 
             nc.vector.scalar_tensor_tensor(mean[:, c], step[:, c], 0.5, v1[:, c], ALU.mult, ALU.add)
         for h in range(2):
             nc.vector.tensor_tensor(rest[:, parts[h]], vv[:].indirect(p2[:, h * V // 32 : (h + 1) * V // 32]), mean[:, parts[h]], ALU.subtract)
+        nc.vector.scalar_tensor_tensor(gated_mean[:], own_tanh[:], 1.0, mean[:], ALU.add, ALU.mult)
+        nc.vector.scalar_tensor_tensor(gated_rest[:], own_tanh[:], 1.0, rest[:], ALU.add, ALU.mult)
         for c in parts:
-            nc.vector.tensor_tensor(pull[:, c], rest[:, c], half_w2[:, c], ALU.mult)
+            nc.vector.tensor_tensor(pull[:, c], gated_rest[:, c], half_w2[:, c], ALU.mult)
         for c in parts:
-            nc.vector.scalar_tensor_tensor(half_mix[:, c], mean[:, c], 0.5, pull[:, c], ALU.mult, ALU.add)
-        for c in parts:
-            nc.vector.scalar_tensor_tensor(result[:, c], own_tanh[:, c], 1.0, half_mix[:, c], ALU.add, ALU.mult)
+            nc.vector.scalar_tensor_tensor(result[:, c], gated_mean[:, c], 0.5, pull[:, c], ALU.mult, ALU.add)
             nc.sync.dma_start(out[:, c], result[:, c])

@@ -44,8 +44,8 @@ def tile_picked_yaft_aft_p_kernel(tc, x_words, x_scales, w1, w2, w3, pos, offs, 
             rows = w.rearrange("(g p t) m -> g p (t m)", g=PASSES, t=PACK)
             nc.sync.dma_start(tile, rows[g])
 
-        def round_pass(copy, rounded, raw):
-            copy(rounded.rearrange("p (c i t) -> p c t i", i=4, t=PACK), raw.rearrange("p (t c i) -> p c t i", t=PACK, i=4))
+        def round_pass(copy, rounded, raw, groups=slice(0, N // 4)):
+            copy(rounded.rearrange("p (c i t) -> p c t i", i=4, t=PACK)[:, groups], raw.rearrange("p (t c i) -> p c t i", t=PACK, i=4)[:, groups])
 
         def quantize_weight(rounded, name, tag=""):
             width = rounded.shape[1] // PACK
@@ -72,6 +72,10 @@ def tile_picked_yaft_aft_p_kernel(tc, x_words, x_scales, w1, w2, w3, pos, offs, 
         x_planes = sb.tile([P, T], U8, name="x_planes", align_bytes=64)
         nc.vector.memset(x_planes[:].bitcast(I32), 0)
 
+        gap_rows = sb.tile([P, D, P], F32, name="gap_rows", align_bytes=64)
+        nc.gpsimd.memset(gap_rows[:], 0.0)
+        bias_rows = sb.tile([P, D, P], F32, name="bias_rows", align_bytes=64)
+        nc.scalar.dma_start(bias_rows[0:2], pos[:, 0, :].rearrange("d (c v) -> c d v", c=2))
         offs_t = load_list(offs, "offs_t")
         words0 = load_words(0)
         for q in range(4):
@@ -84,27 +88,36 @@ def tile_picked_yaft_aft_p_kernel(tc, x_words, x_scales, w1, w2, w3, pos, offs, 
         for g in range(PASSES):
             load_weight(w1_raw[g][:], w1, g)
         words1 = load_words(1)
-        w2_raw = [raw_pass("w2_raw_%d" % g) for g in range(PASSES)]
+        w3_raw = [raw_pass("w3_raw_0"), reuse.tile([P, PACK * N], F32, name="w3_raw_1", offset=0, align_bytes=64)]
+        w2_raw = [raw_pass("w2_raw_0"), reuse.tile([P, PACK * N], F32, name="w2_raw_1", offset=4096, align_bytes=64)]
         for g in range(PASSES):
-            load_weight(w2_raw[g][:], w2, g)
+            load_weight(w3_raw[g][:], w3, g)
+        load_weight(w2_raw[0][:], w2, 0)
         p1 = load_list(pos2, "p1")
+        load_weight(w2_raw[1][:], w2, 1)
         p2 = load_list(pos3, "p2")
         p0 = load_list(pos1, "p0")
-        w3_raw = reuse.tile([P, PASSES, PACK * N], F32, name="w3_raw", offset=0, align_bytes=64)
-        for g in range(PASSES):
-            load_weight(w3_raw[:, g, :], w3, g)
-        bias = sb.tile([P, D, 2], F32, name="bias", align_bytes=64)
-        with nc.allow_non_contiguous_dma(reason="one bias value a partition"):
-            nc.sync.dma_start(bias[:].rearrange("v d c -> v (d c)"),
-                              pos.rearrange("d p (c v) -> (d p c) v", c=2)[0 : D * P * 2 : P + 1, :].rearrange("j v -> v j"))
         own_t = load_list(own, "own_t")
 
         identity = sb.tile([P, P], F32, name="identity", align_bytes=64)
         make_identity(nc, identity[:])
 
+        def turn(acc, src, start, stop):
+            nc.tensor.matmul(acc, src, identity[:], start=start, stop=stop, is_transpose=True)
+
+        nc.vector.tensor_tensor(gap_rows[0:2, 0:2, :], bias_rows[0:2, 0:2, :], bias_rows[0:2, 2:3, :].to_broadcast([2, 2, P]), ALU.subtract)
+        gap01_row = sb.tile([P, P], F32, name="gap01_row", align_bytes=64)
+        nc.vector.tensor_tensor(gap01_row[0:2, :], bias_rows[0:2, 0, :], bias_rows[0:2, 1, :], ALU.subtract)
+        nc.vector.tensor_scalar(gap_rows[0:2, 2, :], gap01_row[0:2, :], 0.5, None, ALU.mult)
+        gaps_t = psum.tile([P, D, P], F32, name="gaps_t", tag="k12_t")
+        for j in range(D):
+            turn(gaps_t[:, j, :], gap_rows[:, j, :], True, True)
+        gaps = sb.tile([P, D, 2], F32, name="gaps", align_bytes=64)
+        nc.scalar.copy(gaps[:], gaps_t[:, :, 0:2])
+
         picked_scales = sb.tile([P, S], U8, name="picked_scales", align_bytes=64)
         picked_words = [sb.tile([P, S], U32, name="picked_words_0", align_bytes=64)]
-        halves = [slice(h * HALF, (h + 1) * HALF) for h in range(2)]
+        pieces = [slice(0, HALF), slice(HALF, HALF + P), slice(HALF + P, S)]
         parts = [slice(c * P, (c + 1) * P) for c in range(2)]
 
         w1_bf = [sb.tile([P, PACK * N], BF16, name="w1_bf16_%d" % g, align_bytes=64) for g in range(PASSES)]
@@ -114,70 +127,70 @@ def tile_picked_yaft_aft_p_kernel(tc, x_words, x_scales, w1, w2, w3, pos, offs, 
         nc.vector.tensor_copy(picked_scales[:], x_planes[:].indirect(offs_t[:]))
         w1_q = quantize_weight(w1_bf[0], "w1a") + quantize_weight(w1_bf[1], "w1b", "w1b_codes")
         picked_words.append(sb.tile([P, S], U32, name="picked_words_1", tag="w1_raw_1", align_bytes=64))
-        for h in range(2):
-            nc.vector.tensor_copy(picked_words[1][:, halves[h]], words1[:].indirect(offs_t[:, h * HALF // 16 : (h + 1) * HALF // 16]))
-        w2_bf = sb.tile([P, PASSES * PACK * N], BF16, name="w2_bf16", tag="w2_bf16", align_bytes=64)
-        round_pass(nc.scalar.copy, w2_bf[:, : PACK * N], w2_raw[0][:])
-        round_pass(nc.vector.tensor_copy, w2_bf[:, PACK * N :], w2_raw[1][:])
-        w2_q = quantize_weight(w2_bf, "w2")
+        for cols in pieces:
+            nc.vector.tensor_copy(picked_words[1][:, cols], words1[:].indirect(offs_t[:, cols.start // 16 : cols.stop // 16]))
+        w2_bf = [sb.tile([P, PACK * N], BF16, name="w2_bf16_%d" % g, align_bytes=64) for g in range(PASSES)]
+        w3_bf = [sb.tile([P, PACK * N], BF16, name="w3_bf16_%d" % g, align_bytes=64) for g in range(PASSES)]
+        round_pass(nc.scalar.copy, w3_bf[0][:], w3_raw[0][:])
+        round_pass(nc.scalar.copy, w3_bf[1][:], w3_raw[1][:], slice(0, N // 8))
+        round_pass(nc.vector.tensor_copy, w3_bf[1][:], w3_raw[1][:], slice(N // 8, N // 4))
+        w3_q = quantize_weight(w3_bf[0], "w3a") + quantize_weight(w3_bf[1], "w3b")
+        round_pass(nc.vector.tensor_copy, w2_bf[0][:], w2_raw[0][:])
+        w2_q = quantize_weight(w2_bf[0], "w2a")
 
-        kk = sb.tile([P, S], F32, name="kk", tag="w2_raw_0", align_bytes=64)
-        kk_acc = [psum.tile([P, HALF], F32, name="kk_acc_%d" % h, tag="kk_acc_%d" % h) for h in range(2)]
-        for g in range(PASSES):
-            for h in range(2):
-                product_pass(kk_acc[h], w1_q, g, halves[h])
-        for h in range(2):
-            nc.scalar.copy(kk[:, halves[h]], kk_acc[h][:])
-        vv_acc = psum.tile([P, S], F32, name="vv_acc", tag="vv_acc")
-        for g in range(PASSES):
-            product_pass(vv_acc, w2_q, g, slice(0, S))
-
-        w3_bf = sb.tile([P, PASSES * PACK * N], BF16, name="w3_bf16", tag="w1b_codes", align_bytes=64)
-        for g in range(PASSES):
-            round_pass(nc.scalar.copy, w3_bf[:, g * PACK * N : (g + 1) * PACK * N], w3_raw[:, g, :])
-
-        k1 = sb.tile([P, V], F32, name="k1", tag="w2_bf16", align_bytes=64)
-        k2 = values("k2")
-        nc.vector.tensor_copy(k1[:], kk[:].indirect(p1[:]))
-        nc.vector.tensor_copy(k2[:], kk[:].indirect(p2[:]))
-        w3_q = quantize_weight(w3_bf, "w3", "w3_codes")
+        kk = reuse.tile([P, S], F32, name="kk", offset=0, align_bytes=64)
+        kk_acc = [psum.tile([P, cols.stop - cols.start], F32, name="kk_acc_%d" % h, tag="kk_acc_%d" % h) for h, cols in enumerate(pieces)]
+        for h, cols in enumerate(pieces):
+            product_pass(kk_acc[h], w1_q, 0, cols)
+        warm = psum.tile([P, S], F32, name="warm", tag="gate_acc")
+        for cols in pieces[:2]:
+            codes, scales = w1_q[0]
+            nc.tensor.matmul_mx(out=warm[:, cols], lhsT=codes.bitcast(FP8X4), lhsT_scale=scales,
+                                rhs=picked_words[0][:, cols].bitcast(FP8X4), rhs_scale=picked_scales[0:P, cols],
+                                start=True, stop=True)
+        for h, cols in enumerate(pieces):
+            product_pass(kk_acc[h], w1_q, 1, cols)
+        for h, cols in enumerate(pieces):
+            nc.scalar.copy(kk[:, cols], kk_acc[h][:])
         gate_acc = psum.tile([P, S], F32, name="gate_acc", tag="gate_acc")
         for g in range(PASSES):
             product_pass(gate_acc, w3_q, g, slice(0, S))
-        vv = reuse.tile([P, S], F32, name="vv", offset=0, align_bytes=64)
-        nc.scalar.copy(vv[:], vv_acc[:])
-        gate_tanh = sb.tile([P, S], F32, name="gate_tanh", align_bytes=64)
+        vv_acc = psum.tile([P, S], F32, name="vv_acc", tag="vv_acc")
+        product_pass(vv_acc, w2_q, 0, slice(0, S))
+        round_pass(nc.scalar.copy, w2_bf[1][:], w2_raw[1][:])
+        gate_tanh = reuse.tile([P, S], F32, name="gate_tanh", offset=5184, align_bytes=64)
         nc.scalar.activation(gate_tanh[:], gate_acc[:], ACT.Tanh, scale=0.5)
 
-        k12 = reuse.tile([P, V], F32, name="k12", offset=2048, align_bytes=64)
-        gaps = reuse.tile([P, 2, 2, 2], F32, name="gaps", offset=3072, align_bytes=64)
-        k01 = reuse.tile([P, V], F32, name="k01", offset=3136, align_bytes=64)
-        half_gap01 = sb.tile([P, 2], F32, name="half_gap01", align_bytes=64)
-        nc.vector.tensor_tensor(gaps[:], bias[:, 0:2, :].unsqueeze(2).to_broadcast([P, 2, 2, 2]),
-                                bias[:, 1:3, :].unsqueeze(1).to_broadcast([P, 2, 2, 2]), ALU.subtract)
-        nc.vector.tensor_tensor(k12[:], k1[:], k2[:], ALU.subtract)
-        nc.vector.tensor_scalar(half_gap01[:], gaps[:, 0, 0, :], 0.5, None, ALU.mult)
+        k1, minus_k2 = values("k1"), values("minus_k2")
+        k2 = reuse.tile([P, V], F32, name="k2", offset=3136, align_bytes=64)
+        k01 = reuse.tile([P, V], F32, name="k01", offset=4160, align_bytes=64)
+        nc.vector.tensor_copy(k1[:], kk[:].indirect(p1[:]))
+        w2_q = w2_q + quantize_weight(w2_bf[1], "w2b")
+        product_pass(vv_acc, w2_q, 1, slice(0, S))
+        nc.vector.tensor_copy(k2[:], kk[:].indirect(p2[:]))
+        nc.scalar.mul(minus_k2[:], k2[:], -1.0)
+        vv = sb.tile([P, S], F32, name="vv", align_bytes=64)
+        nc.scalar.copy(vv[:], vv_acc[:])
         for c in range(2):
             nc.vector.tensor_tensor(k01[:, parts[c]], kk[:].indirect(p0[:, c * P // 16 : (c + 1) * P // 16]), k1[:, parts[c]], ALU.subtract)
 
-        def turn(acc, src, start, stop):
-            nc.tensor.matmul(acc, src, identity[:], start=start, stop=stop, is_transpose=True)
-
-        k12_t = psum.tile([P, V], F32, name="k12_t")
-        k01_t = [psum.tile([P, P], F32, name="k01_t_%d" % c) for c in range(2)]
+        k12_t = psum.tile([P, V], F32, name="k12_t", tag="k12_t")
+        k01_t = [psum.tile([P, P], F32, name="k01_t_%d" % c, tag=("kk_acc_2", "k01_t")[c]) for c in range(2)]
         k02_t = [psum.tile([P, P], F32, name="k02_t_%d" % c, tag="kk_acc_%d" % c) for c in range(2)]
         e12_t, e02_t, t01_t = values("e12_t"), values("e02_t"), values("t01_t")
         for c in range(2):
-            turn(k12_t[:, parts[c]], k12[:, parts[c]], True, True)
+            turn(k12_t[:, parts[c]], k1[:, parts[c]], True, False)
+            turn(k12_t[:, parts[c]], minus_k2[:, parts[c]], False, True)
         for c in range(2):
-            turn(k02_t[c][:], k12[:, parts[c]], True, False)
+            turn(k02_t[c][:], k1[:, parts[c]], True, False)
+            turn(k02_t[c][:], minus_k2[:, parts[c]], False, False)
         for c in range(2):
-            nc.scalar.activation(e12_t[:, parts[c]], k12_t[:, parts[c]], ACT.Exp, bias=gaps[:, 1, 1, c : c + 1])
+            nc.scalar.activation(e12_t[:, parts[c]], k12_t[:, parts[c]], ACT.Exp, bias=gaps[:, 1, c : c + 1])
         for c in range(2):
             turn(k01_t[c][:], k01[:, parts[c]], True, True)
             turn(k02_t[c][:], k01[:, parts[c]], False, True)
-            nc.scalar.activation(t01_t[:, parts[c]], k01_t[c][:], ACT.Tanh, bias=half_gap01[:, c : c + 1], scale=0.5)
-            nc.scalar.activation(e02_t[:, parts[c]], k02_t[c][:], ACT.Exp, bias=gaps[:, 0, 1, c : c + 1])
+            nc.scalar.activation(t01_t[:, parts[c]], k01_t[c][:], ACT.Tanh, bias=gaps[:, 2, c : c + 1], scale=0.5)
+            nc.scalar.activation(e02_t[:, parts[c]], k02_t[c][:], ACT.Exp, bias=gaps[:, 0, c : c + 1])
         t01 = psum.tile([P, V], F32, name="t01", tag="vv_acc")
         for c in range(2):
             turn(t01[:, parts[c]], t01_t[:, parts[c]], True, True)
@@ -191,12 +204,15 @@ def tile_picked_yaft_aft_p_kernel(tc, x_words, x_scales, w1, w2, w3, pos, offs, 
         for c in parts:
             nc.scalar.activation(half_w2[:, c], root[:, c], ACT.Square)
 
-        v1, dv, own_tanh = values("v1"), values("dv"), values("own_tanh")
+        own_tanh = reuse.tile([P, V], F32, name="own_tanh", offset=3136, align_bytes=64)
+        v1, dv = values("v1"), values("dv")
         step, mean, rest, pull, result = values("step"), values("mean"), values("rest"), values("pull"), values("result")
         gated_mean, gated_rest = values("gated_mean"), values("gated_rest")
-        nc.vector.tensor_copy(v1[:], vv[:].indirect(p1[:]))
         nc.vector.tensor_copy(own_tanh[:], gate_tanh[:].indirect(own_t[:]))
-        nc.vector.tensor_tensor(dv[:], vv[:].indirect(p0[:]), v1[:], ALU.subtract)
+        for c in range(2):
+            nc.vector.tensor_copy(v1[:, parts[c]], vv[:].indirect(p1[:, c * P // 16 : (c + 1) * P // 16]))
+        for c in range(2):
+            nc.vector.tensor_tensor(dv[:, parts[c]], vv[:].indirect(p0[:, c * P // 16 : (c + 1) * P // 16]), v1[:, parts[c]], ALU.subtract)
         for c in parts:
             nc.vector.scalar_tensor_tensor(step[:, c], t01[:, c], 1.0, dv[:, c], ALU.add, ALU.mult)
         for c in parts:
@@ -204,7 +220,8 @@ def tile_picked_yaft_aft_p_kernel(tc, x_words, x_scales, w1, w2, w3, pos, offs, 
         for h in range(2):
             nc.vector.tensor_tensor(rest[:, parts[h]], vv[:].indirect(p2[:, h * V // 32 : (h + 1) * V // 32]), mean[:, parts[h]], ALU.subtract)
         nc.vector.scalar_tensor_tensor(gated_mean[:], own_tanh[:], 1.0, mean[:], ALU.add, ALU.mult)
-        nc.vector.scalar_tensor_tensor(gated_rest[:], own_tanh[:], 1.0, rest[:], ALU.add, ALU.mult)
+        for c in parts:
+            nc.vector.scalar_tensor_tensor(gated_rest[:, c], own_tanh[:, c], 1.0, rest[:, c], ALU.add, ALU.mult)
         for c in parts:
             nc.vector.tensor_tensor(pull[:, c], gated_rest[:, c], half_w2[:, c], ALU.mult)
         for c in parts:

@@ -142,12 +142,6 @@ def tile_picked_yaft_aft_p_kernel(tc, x_words, x_scales, w1, w2, w3, pos, offs, 
         kk_acc = [psum.tile([P, cols.stop - cols.start], F32, name="kk_acc_%d" % h, tag="kk_acc_%d" % h) for h, cols in enumerate(pieces)]
         for h, cols in enumerate(pieces):
             product_pass(kk_acc[h], w1_q, 0, cols)
-        warm = psum.tile([P, S], F32, name="warm", tag="gate_acc")
-        for cols in pieces[:2]:
-            codes, scales = w1_q[0]
-            nc.tensor.matmul_mx(out=warm[:, cols], lhsT=codes.bitcast(FP8X4), lhsT_scale=scales,
-                                rhs=picked_words[0][:, cols].bitcast(FP8X4), rhs_scale=picked_scales[0:P, cols],
-                                start=True, stop=True)
         for h, cols in enumerate(pieces):
             product_pass(kk_acc[h], w1_q, 1, cols)
         for h, cols in enumerate(pieces):

@@ -93,9 +93,9 @@ def tile_picked_yaft_aft_p_kernel(tc, x_words, x_scales, w1, w2, w3, pos, offs, 
         for g in range(PASSES):
             load_weight(w3_raw[g][:], w3, g)
         load_weight(w2_raw[0][:], w2, 0)
-        p1 = load_list(pos2, "p1")
-        load_weight(w2_raw[1][:], w2, 1)
         p2 = load_list(pos3, "p2")
+        load_weight(w2_raw[1][:], w2, 1)
+        p1 = load_list(pos2, "p1")
         p0 = load_list(pos1, "p0")
         own_t = load_list(own, "own_t")
 
@@ -149,43 +149,49 @@ def tile_picked_yaft_aft_p_kernel(tc, x_words, x_scales, w1, w2, w3, pos, offs, 
         gate_acc = psum.tile([P, S], F32, name="gate_acc", tag="gate_acc")
         for g in range(PASSES):
             product_pass(gate_acc, w3_q, g, slice(0, S))
-        vv_acc = psum.tile([P, S], F32, name="vv_acc", tag="vv_acc")
-        product_pass(vv_acc, w2_q, 0, slice(0, S))
+        shares = [slice(0, HALF), slice(HALF, S)]
+        vv_acc = [psum.tile([P, HALF], F32, name="vv_acc_%d" % h, tag="vv_acc_%d" % h) for h in range(2)]
+        for h in range(2):
+            product_pass(vv_acc[h], w2_q, 0, shares[h])
         round_pass(nc.scalar.copy, w2_bf[1][:], w2_raw[1][:])
         gate_tanh = reuse.tile([P, S], F32, name="gate_tanh", offset=5184, align_bytes=64)
         nc.scalar.activation(gate_tanh[:], gate_acc[:], ACT.Tanh, scale=0.5)
 
-        k1, minus_k2 = values("k1"), values("minus_k2")
-        k2 = reuse.tile([P, V], F32, name="k2", offset=3136, align_bytes=64)
-        k01 = reuse.tile([P, V], F32, name="k01", offset=4160, align_bytes=64)
-        nc.vector.tensor_copy(k1[:], kk[:].indirect(p1[:]))
-        w2_q = w2_q + quantize_weight(w2_bf[1], "w2b")
-        product_pass(vv_acc, w2_q, 1, slice(0, S))
+        k2 = sb.tile([P, V], F32, name="k2", tag="k2", align_bytes=64)
+        minus_k2 = reuse.tile([P, V], F32, name="minus_k2", offset=3136, align_bytes=64)
+        k1 = [values("k1_a"), reuse.tile([P, P], F32, name="k1_b", offset=4160, align_bytes=64)]
+        k01 = [reuse.tile([P, P], F32, name="k01_a", offset=4672, align_bytes=64), values("k01_b")]
         nc.vector.tensor_copy(k2[:], kk[:].indirect(p2[:]))
         nc.scalar.mul(minus_k2[:], k2[:], -1.0)
+        nc.vector.tensor_copy(k1[0][:, :P], kk[:].indirect(p1[:, : P // 16]))
+        w2_q = w2_q + quantize_weight(w2_bf[1], "w2b")
+        for h in range(2):
+            product_pass(vv_acc[h], w2_q, 1, shares[h])
+        nc.vector.tensor_copy(k1[1][:, :P], kk[:].indirect(p1[:, P // 16 :]))
         vv = sb.tile([P, S], F32, name="vv", align_bytes=64)
-        nc.scalar.copy(vv[:], vv_acc[:])
+        for h in range(2):
+            nc.scalar.copy(vv[:, shares[h]], vv_acc[h][:])
         for c in range(2):
-            nc.vector.tensor_tensor(k01[:, parts[c]], kk[:].indirect(p0[:, c * P // 16 : (c + 1) * P // 16]), k1[:, parts[c]], ALU.subtract)
+            nc.vector.tensor_tensor(k01[c][:, :P], kk[:].indirect(p0[:, c * P // 16 : (c + 1) * P // 16]), k1[c][:, :P], ALU.subtract)
 
         k12_t = psum.tile([P, V], F32, name="k12_t", tag="k12_t")
         k01_t = [psum.tile([P, P], F32, name="k01_t_%d" % c, tag=("kk_acc_2", "k01_t")[c]) for c in range(2)]
         k02_t = [psum.tile([P, P], F32, name="k02_t_%d" % c, tag="kk_acc_%d" % c) for c in range(2)]
         e12_t, e02_t, t01_t = values("e12_t"), values("e02_t"), values("t01_t")
         for c in range(2):
-            turn(k12_t[:, parts[c]], k1[:, parts[c]], True, False)
+            turn(k12_t[:, parts[c]], k1[c][:, :P], True, False)
             turn(k12_t[:, parts[c]], minus_k2[:, parts[c]], False, True)
         for c in range(2):
-            turn(k02_t[c][:], k1[:, parts[c]], True, False)
+            turn(k02_t[c][:], k1[c][:, :P], True, False)
             turn(k02_t[c][:], minus_k2[:, parts[c]], False, False)
         for c in range(2):
             nc.scalar.activation(e12_t[:, parts[c]], k12_t[:, parts[c]], ACT.Exp, bias=gaps[:, 1, c : c + 1])
         for c in range(2):
-            turn(k01_t[c][:], k01[:, parts[c]], True, True)
-            turn(k02_t[c][:], k01[:, parts[c]], False, True)
+            turn(k01_t[c][:], k01[c][:, :P], True, True)
+            turn(k02_t[c][:], k01[c][:, :P], False, True)
             nc.scalar.activation(t01_t[:, parts[c]], k01_t[c][:], ACT.Tanh, bias=gaps[:, 2, c : c + 1], scale=0.5)
             nc.scalar.activation(e02_t[:, parts[c]], k02_t[c][:], ACT.Exp, bias=gaps[:, 0, c : c + 1])
-        t01 = psum.tile([P, V], F32, name="t01", tag="vv_acc")
+        t01 = psum.tile([P, V], F32, name="t01", tag="vv_acc_0")
         for c in range(2):
             turn(t01[:, parts[c]], t01_t[:, parts[c]], True, True)
         e_sum = psum.tile([P, V], F32, name="e_sum", tag="gate_acc")
@@ -198,7 +204,7 @@ def tile_picked_yaft_aft_p_kernel(tc, x_words, x_scales, w1, w2, w3, pos, offs, 
         for c in parts:
             nc.scalar.activation(half_w2[:, c], root[:, c], ACT.Square)
 
-        own_tanh = reuse.tile([P, V], F32, name="own_tanh", offset=3136, align_bytes=64)
+        own_tanh = sb.tile([P, V], F32, name="own_tanh", tag="k2", align_bytes=64)
         v1, dv = values("v1"), values("dv")
         step, mean, rest, pull, result = values("step"), values("mean"), values("rest"), values("pull"), values("result")
         gated_mean, gated_rest = values("gated_mean"), values("gated_rest")

@@ -93,9 +93,9 @@ def tile_picked_yaft_aft_p_kernel(tc, x_words, x_scales, w1, w2, w3, pos, offs, 
         for g in range(PASSES):
             load_weight(w3_raw[g][:], w3, g)
         load_weight(w2_raw[0][:], w2, 0)
-        p2 = load_list(pos3, "p2")
-        load_weight(w2_raw[1][:], w2, 1)
         p1 = load_list(pos2, "p1")
+        load_weight(w2_raw[1][:], w2, 1)
+        p2 = load_list(pos3, "p2")
         p0 = load_list(pos1, "p0")
         own_t = load_list(own, "own_t")
 
@@ -154,20 +154,18 @@ def tile_picked_yaft_aft_p_kernel(tc, x_words, x_scales, w1, w2, w3, pos, offs, 
         for h in range(2):
             product_pass(vv_acc[h], w2_q, 0, shares[h])
         round_pass(nc.scalar.copy, w2_bf[1][:], w2_raw[1][:])
+        minus_k2 = reuse.tile([P, V], F32, name="minus_k2", offset=3136, align_bytes=64)
+        nc.scalar.activation(minus_k2[:], kk[:].indirect(p2[:]), ACT.Copy, scale=-1.0)
         gate_tanh = reuse.tile([P, S], F32, name="gate_tanh", offset=5184, align_bytes=64)
         nc.scalar.activation(gate_tanh[:], gate_acc[:], ACT.Tanh, scale=0.5)
 
-        k2 = sb.tile([P, V], F32, name="k2", tag="k2", align_bytes=64)
-        minus_k2 = reuse.tile([P, V], F32, name="minus_k2", offset=3136, align_bytes=64)
-        k1 = [values("k1_a"), reuse.tile([P, P], F32, name="k1_b", offset=4160, align_bytes=64)]
+        k1 = [values("k1_a"), values("k1_b")]
         k01 = [reuse.tile([P, P], F32, name="k01_a", offset=4672, align_bytes=64), values("k01_b")]
-        nc.vector.tensor_copy(k2[:], kk[:].indirect(p2[:]))
-        nc.scalar.mul(minus_k2[:], k2[:], -1.0)
         nc.vector.tensor_copy(k1[0][:, :P], kk[:].indirect(p1[:, : P // 16]))
+        nc.vector.tensor_copy(k1[1][:, :P], kk[:].indirect(p1[:, P // 16 :]))
         w2_q = w2_q + quantize_weight(w2_bf[1], "w2b")
         for h in range(2):
             product_pass(vv_acc[h], w2_q, 1, shares[h])
-        nc.vector.tensor_copy(k1[1][:, :P], kk[:].indirect(p1[:, P // 16 :]))
         vv = sb.tile([P, S], F32, name="vv", align_bytes=64)
         for h in range(2):
             nc.scalar.copy(vv[:, shares[h]], vv_acc[h][:])
@@ -204,7 +202,7 @@ def tile_picked_yaft_aft_p_kernel(tc, x_words, x_scales, w1, w2, w3, pos, offs, 
         for c in parts:
             nc.scalar.activation(half_w2[:, c], root[:, c], ACT.Square)
 
-        own_tanh = sb.tile([P, V], F32, name="own_tanh", tag="k2", align_bytes=64)
+        own_tanh = sb.tile([P, V], F32, name="own_tanh", align_bytes=64)
         v1, dv = values("v1"), values("dv")
         step, mean, rest, pull, result = values("step"), values("mean"), values("rest"), values("pull"), values("result")
         gated_mean, gated_rest = values("gated_mean"), values("gated_rest")

@@ -88,14 +88,14 @@ def tile_picked_yaft_aft_p_kernel(tc, x_words, x_scales, w1, w2, w3, pos, offs, 
         for g in range(PASSES):
             load_weight(w1_raw[g][:], w1, g)
         words1 = load_words(1)
-        w3_raw = [raw_pass("w3_raw_0"), reuse.tile([P, PACK * N], F32, name="w3_raw_1", offset=0, align_bytes=64)]
-        w2_raw = [raw_pass("w2_raw_0"), reuse.tile([P, PACK * N], F32, name="w2_raw_1", offset=4096, align_bytes=64)]
-        for g in range(PASSES):
-            load_weight(w3_raw[g][:], w3, g)
-        load_weight(w2_raw[0][:], w2, 0)
-        p1 = load_list(pos2, "p1")
-        load_weight(w2_raw[1][:], w2, 1)
+        w3_raw = [raw_pass("w3_raw_0"), raw_pass("w3_raw_1")]
+        w2_raw = [raw_pass("w2_raw_0"), reuse.tile([P, PACK * N], F32, name="w2_raw_1", offset=1024, align_bytes=64)]
         p2 = load_list(pos3, "p2")
+        load_weight(w3_raw[0][:], w3, 0)
+        load_weight(w3_raw[1][:], w3, 1)
+        load_weight(w2_raw[0][:], w2, 0)
+        load_weight(w2_raw[1][:], w2, 1)
+        p1 = load_list(pos2, "p1")
         p0 = load_list(pos1, "p0")
         own_t = load_list(own, "own_t")
 
@@ -132,13 +132,15 @@ def tile_picked_yaft_aft_p_kernel(tc, x_words, x_scales, w1, w2, w3, pos, offs, 
         w2_bf = [sb.tile([P, PACK * N], BF16, name="w2_bf16_%d" % g, align_bytes=64) for g in range(PASSES)]
         w3_bf = [sb.tile([P, PACK * N], BF16, name="w3_bf16_%d" % g, align_bytes=64) for g in range(PASSES)]
         round_pass(nc.scalar.copy, w3_bf[0][:], w3_raw[0][:])
-        round_pass(nc.scalar.copy, w3_bf[1][:], w3_raw[1][:], slice(0, N // 8))
-        round_pass(nc.vector.tensor_copy, w3_bf[1][:], w3_raw[1][:], slice(N // 8, N // 4))
-        w3_q = quantize_weight(w3_bf[0], "w3a") + quantize_weight(w3_bf[1], "w3b")
+        round_pass(nc.scalar.copy, w3_bf[1][:], w3_raw[1][:], slice(0, 3 * N // 16))
+        round_pass(nc.vector.tensor_copy, w3_bf[1][:], w3_raw[1][:], slice(3 * N // 16, N // 4))
+        w3_q = quantize_weight(w3_bf[0], "w3a")
         round_pass(nc.vector.tensor_copy, w2_bf[0][:], w2_raw[0][:])
+        w3_q = w3_q + quantize_weight(w3_bf[1], "w3b")
         w2_q = quantize_weight(w2_bf[0], "w2a")
+        round_pass(nc.vector.tensor_copy, w2_bf[1][:], w2_raw[1][:], slice(N // 8, N // 4))
 
-        kk = reuse.tile([P, S], F32, name="kk", offset=0, align_bytes=64)
+        kk = sb.tile([P, S], F32, name="kk", tag="w3_raw_1", align_bytes=64)
         kk_acc = [psum.tile([P, cols.stop - cols.start], F32, name="kk_acc_%d" % h, tag="kk_acc_%d" % h) for h, cols in enumerate(pieces)]
         for h, cols in enumerate(pieces):
             product_pass(kk_acc[h], w1_q, 0, cols)
@@ -149,49 +151,56 @@ def tile_picked_yaft_aft_p_kernel(tc, x_words, x_scales, w1, w2, w3, pos, offs, 
         gate_acc = psum.tile([P, S], F32, name="gate_acc", tag="gate_acc")
         for g in range(PASSES):
             product_pass(gate_acc, w3_q, g, slice(0, S))
-        shares = [slice(0, HALF), slice(HALF, S)]
-        vv_acc = [psum.tile([P, HALF], F32, name="vv_acc_%d" % h, tag="vv_acc_%d" % h) for h in range(2)]
-        for h in range(2):
-            product_pass(vv_acc[h], w2_q, 0, shares[h])
-        round_pass(nc.scalar.copy, w2_bf[1][:], w2_raw[1][:])
-        minus_k2 = reuse.tile([P, V], F32, name="minus_k2", offset=3136, align_bytes=64)
-        nc.scalar.activation(minus_k2[:], kk[:].indirect(p2[:]), ACT.Copy, scale=-1.0)
-        gate_tanh = reuse.tile([P, S], F32, name="gate_tanh", offset=5184, align_bytes=64)
-        nc.scalar.activation(gate_tanh[:], gate_acc[:], ACT.Tanh, scale=0.5)
 
-        k1 = [values("k1_a"), values("k1_b")]
-        k01 = [reuse.tile([P, P], F32, name="k01_a", offset=4672, align_bytes=64), values("k01_b")]
-        nc.vector.tensor_copy(k1[0][:, :P], kk[:].indirect(p1[:, : P // 16]))
-        nc.vector.tensor_copy(k1[1][:, :P], kk[:].indirect(p1[:, P // 16 :]))
-        w2_q = w2_q + quantize_weight(w2_bf[1], "w2b")
-        for h in range(2):
-            product_pass(vv_acc[h], w2_q, 1, shares[h])
-        vv = sb.tile([P, S], F32, name="vv", align_bytes=64)
-        for h in range(2):
-            nc.scalar.copy(vv[:, shares[h]], vv_acc[h][:])
+        def slice_of(offsets, c):
+            return offsets[:, c * P // 16 : (c + 1) * P // 16]
+
+        round_pass(nc.scalar.copy, w2_bf[1][:], w2_raw[1][:], slice(0, N // 8))
+        minus_k2 = values("minus_k2")
+        nc.scalar.activation(minus_k2[:], kk[:].indirect(p2[:]), ACT.Copy, scale=-1.0)
+        gate_tanh = sb.tile([P, S], F32, name="gate_tanh", align_bytes=64)
+        nc.scalar.activation(gate_tanh[:], gate_acc[:], ACT.Tanh, scale=0.5)
+        k1 = [sb.tile([P, P], F32, name="k1_0", align_bytes=64), reuse.tile([P, P], F32, name="k1_1", offset=1280, align_bytes=64)]
+        nc.vector.tensor_copy(k1[0][:], kk[:].indirect(slice_of(p1, 0)))
+        w2_q = w2_q + quantize_weight(w2_bf[1], "w2b", "w2b_codes")
+        nc.vector.tensor_copy(k1[1][:], kk[:].indirect(slice_of(p1, 1)))
+        k01 = reuse.tile([P, V], F32, name="k01", offset=256, align_bytes=64)
         for c in range(2):
-            nc.vector.tensor_tensor(k01[c][:, :P], kk[:].indirect(p0[:, c * P // 16 : (c + 1) * P // 16]), k1[c][:, :P], ALU.subtract)
+            nc.vector.tensor_tensor(k01[:, parts[c]], kk[:].indirect(slice_of(p0, c)), k1[c][:], ALU.subtract)
 
         k12_t = psum.tile([P, V], F32, name="k12_t", tag="k12_t")
         k01_t = [psum.tile([P, P], F32, name="k01_t_%d" % c, tag=("kk_acc_2", "k01_t")[c]) for c in range(2)]
         k02_t = [psum.tile([P, P], F32, name="k02_t_%d" % c, tag="kk_acc_%d" % c) for c in range(2)]
         e12_t, e02_t, t01_t = values("e12_t"), values("e02_t"), values("t01_t")
-        for c in range(2):
-            turn(k12_t[:, parts[c]], k1[c][:, :P], True, False)
+        shares = [slice(0, HALF), slice(HALF, S)]
+        vv_acc = [psum.tile([P, HALF], F32, name="vv_acc_%d" % h, tag="vv_acc_%d" % h) for h in range(2)]
+        for g in range(PASSES):
+            for h in range(2):
+                product_pass(vv_acc[h], w2_q, g, shares[h])
+        vv = sb.tile([P, S], F32, name="vv", align_bytes=64)
+        for h in range(2):
+            nc.scalar.copy(vv[:, shares[h]], vv_acc[h][:])
+        own_tanh = sb.tile([P, V], F32, name="own_tanh", tag="w2b_codes", align_bytes=64)
+        nc.vector.tensor_copy(own_tanh[:, parts[0]], gate_tanh[:].indirect(slice_of(own_t, 0)))
+        nc.scalar.activation(own_tanh[:, parts[1]], gate_tanh[:].indirect(slice_of(own_t, 1)), ACT.Copy)
+        for c in (1, 0):
+            turn(k12_t[:, parts[c]], k1[c][:], True, False)
             turn(k12_t[:, parts[c]], minus_k2[:, parts[c]], False, True)
-        for c in range(2):
-            turn(k02_t[c][:], k1[c][:, :P], True, False)
-            turn(k02_t[c][:], minus_k2[:, parts[c]], False, False)
         for c in range(2):
             nc.scalar.activation(e12_t[:, parts[c]], k12_t[:, parts[c]], ACT.Exp, bias=gaps[:, 1, c : c + 1])
         for c in range(2):
-            turn(k01_t[c][:], k01[c][:, :P], True, True)
-            turn(k02_t[c][:], k01[c][:, :P], False, True)
-            nc.scalar.activation(t01_t[:, parts[c]], k01_t[c][:], ACT.Tanh, bias=gaps[:, 2, c : c + 1], scale=0.5)
-            nc.scalar.activation(e02_t[:, parts[c]], k02_t[c][:], ACT.Exp, bias=gaps[:, 0, c : c + 1])
-        t01 = psum.tile([P, V], F32, name="t01", tag="vv_acc_0")
+            turn(k01_t[c][:], k01[:, parts[c]], True, True)
         for c in range(2):
-            turn(t01[:, parts[c]], t01_t[:, parts[c]], True, True)
+            turn(k02_t[c][:], k01[:, parts[c]], True, False)
+            turn(k02_t[c][:], k1[c][:], False, False)
+            turn(k02_t[c][:], minus_k2[:, parts[c]], False, True)
+        for c in range(2):
+            nc.scalar.activation(t01_t[:, parts[c]], k01_t[c][:], ACT.Tanh, bias=gaps[:, 2, c : c + 1], scale=0.5)
+        for c in range(2):
+            nc.scalar.activation(e02_t[:, parts[c]], k02_t[c][:], ACT.Exp, bias=gaps[:, 0, c : c + 1])
+        t01 = psum.tile([P, V], F32, name="t01", tag="k12_t")
+        for c in parts:
+            turn(t01[:, c], t01_t[:, c], True, True)
         e_sum = psum.tile([P, V], F32, name="e_sum", tag="gate_acc")
         root, half_w2 = values("root"), values("half_w2")
         for c in parts:
@@ -202,21 +211,19 @@ def tile_picked_yaft_aft_p_kernel(tc, x_words, x_scales, w1, w2, w3, pos, offs, 
         for c in parts:
             nc.scalar.activation(half_w2[:, c], root[:, c], ACT.Square)
 
-        own_tanh = sb.tile([P, V], F32, name="own_tanh", align_bytes=64)
         v1, dv = values("v1"), values("dv")
         step, mean, rest, pull, result = values("step"), values("mean"), values("rest"), values("pull"), values("result")
         gated_mean, gated_rest = values("gated_mean"), values("gated_rest")
-        nc.vector.tensor_copy(own_tanh[:], gate_tanh[:].indirect(own_t[:]))
         for c in range(2):
-            nc.vector.tensor_copy(v1[:, parts[c]], vv[:].indirect(p1[:, c * P // 16 : (c + 1) * P // 16]))
+            nc.vector.tensor_copy(v1[:, parts[c]], vv[:].indirect(slice_of(p1, c)))
         for c in range(2):
-            nc.vector.tensor_tensor(dv[:, parts[c]], vv[:].indirect(p0[:, c * P // 16 : (c + 1) * P // 16]), v1[:, parts[c]], ALU.subtract)
+            nc.vector.tensor_tensor(dv[:, parts[c]], vv[:].indirect(slice_of(p0, c)), v1[:, parts[c]], ALU.subtract)
         for c in parts:
             nc.vector.scalar_tensor_tensor(step[:, c], t01[:, c], 1.0, dv[:, c], ALU.add, ALU.mult)
         for c in parts:
             nc.vector.scalar_tensor_tensor(mean[:, c], step[:, c], 0.5, v1[:, c], ALU.mult, ALU.add)
-        for h in range(2):
-            nc.vector.tensor_tensor(rest[:, parts[h]], vv[:].indirect(p2[:, h * V // 32 : (h + 1) * V // 32]), mean[:, parts[h]], ALU.subtract)
+        for c in range(2):
+            nc.vector.tensor_tensor(rest[:, parts[c]], vv[:].indirect(slice_of(p2, c)), mean[:, parts[c]], ALU.subtract)
         nc.vector.scalar_tensor_tensor(gated_mean[:], own_tanh[:], 1.0, mean[:], ALU.add, ALU.mult)
         for c in parts:
             nc.vector.scalar_tensor_tensor(gated_rest[:, c], own_tanh[:, c], 1.0, rest[:, c], ALU.add, ALU.mult)

from contextlib import ExitStack

import concourse.mybir as mybir
from concourse.masks import make_identity

K, T, S, V, N, D = 1024, 1024, 512, 256, 128, 3
FLOPS = 2 * 3 * K * N * S

F32 = mybir.dt.float32
BF16 = mybir.dt.bfloat16
I32 = mybir.dt.int32
U32 = mybir.dt.uint32
U16 = mybir.dt.uint16
U8 = mybir.dt.uint8
FP8X4 = mybir.dt.float8_e4m3fn_x4
ALU = mybir.AluOpType
ACT = mybir.ActivationFunctionType

P = 128
PACK = 4
PASSES = K // (P * PACK)
HALF = S // 2


def tile_picked_yaft_aft_p_kernel(tc, x_words, x_scales, w1, w2, w3, pos, offs, pos1, pos2, pos3, own, out):
    nc = tc.nc
    with ExitStack() as ctx:
        lists = ctx.enter_context(tc.tile_pool(name="lists", bufs=1))
        sb = ctx.enter_context(tc.tile_pool(name="sb", bufs=1))
        reuse = ctx.enter_context(tc.tile_pool(name="reuse", bufs=1))
        psum = ctx.enter_context(tc.psum_pool(name="psum", bufs=1))

        def load_list(src, name):
            tile = lists.tile([P, src.shape[1]], U16, name=name)
            nc.sync.dma_start(tile[:], src)
            return tile

        def load_words(g):
            tile = sb.tile([P, T], U32, name="x_words_%d" % g, align_bytes=64)
            nc.sync.dma_start(tile[:].bitcast(I32), x_words[g].rearrange("p n t -> p (n t)").bitcast(I32))
            return tile

        def load_weight(tile, w, g):
            rows = w.rearrange("(g p t) m -> g p (t m)", g=PASSES, t=PACK)
            nc.sync.dma_start(tile, rows[g])

        def round_pass(copy, rounded, raw, groups=slice(0, N // 4)):
            copy(rounded.rearrange("p (c i t) -> p c t i", i=4, t=PACK)[:, groups], raw.rearrange("p (t c i) -> p c t i", t=PACK, i=4)[:, groups])

        def quantize_weight(rounded, name, tag=""):
            width = rounded.shape[1] // PACK
            codes = sb.tile([P, width], U32, name=name + "_codes", tag=tag, align_bytes=64)
            scales = sb.tile([P, width], U8, name=name + "_scales", align_bytes=64)
            nc.vector.quantize_mx(out=codes[:].bitcast(FP8X4), scales=scales[:], in_=rounded[:])
            return [(codes[:, c : c + N], scales[:, c : c + N]) for c in range(0, width, N)]

        def product_pass(acc, weight, g, cols):
            codes, scales = weight[g]
            nc.tensor.matmul_mx(
                out=acc[:],
                lhsT=codes.bitcast(FP8X4),
                lhsT_scale=scales,
                rhs=picked_words[g][:, cols].bitcast(FP8X4),
                rhs_scale=picked_scales[PACK * g : P, cols],
                start=(g == 0),
                stop=(g == PASSES - 1),
            )

        def values(name):
            return sb.tile([P, V], F32, name=name, align_bytes=64)

        x_planes = sb.tile([P, T], U8, name="x_planes", align_bytes=64)
        nc.vector.memset(x_planes[:].bitcast(I32), 0)

        gap_rows = sb.tile([P, D, P], F32, name="gap_rows", align_bytes=64)
        nc.gpsimd.memset(gap_rows[:], 0.0)
        bias_rows = sb.tile([P, D, P], F32, name="bias_rows", align_bytes=64)
        nc.scalar.dma_start(bias_rows[0:2], pos[:, 0, :].rearrange("d (c v) -> c d v", c=2))
        offs_t = load_list(offs, "offs_t")
        words0 = load_words(0)
        for q in range(4):
            nc.sync.dma_start(x_planes[32 * q : 32 * q + 4 * PASSES, :].bitcast(I32),
                              x_scales[:, 4 * q : 4 * q + 4, :].bitcast(I32))
        def raw_pass(name):
            return sb.tile([P, PACK * N], F32, name=name, tag=name, align_bytes=64)

        w1_raw = [raw_pass("w1_raw_%d" % g) for g in range(PASSES)]
        for g in range(PASSES):
            load_weight(w1_raw[g][:], w1, g)
        words1 = load_words(1)
        w3_raw = [raw_pass("w3_raw_0"), raw_pass("w3_raw_1")]
        w2_raw = [raw_pass("w2_raw_0"), reuse.tile([P, PACK * N], F32, name="w2_raw_1", offset=1024, align_bytes=64)]
        p2 = load_list(pos3, "p2")
        load_weight(w3_raw[0][:], w3, 0)
        load_weight(w3_raw[1][:], w3, 1)
        load_weight(w2_raw[0][:], w2, 0)
        load_weight(w2_raw[1][:], w2, 1)
        p1 = load_list(pos2, "p1")
        p0 = load_list(pos1, "p0")
        own_t = load_list(own, "own_t")

        identity = sb.tile([P, P], F32, name="identity", align_bytes=64)
        make_identity(nc, identity[:])

        def turn(acc, src, start, stop):
            nc.tensor.matmul(acc, src, identity[:], start=start, stop=stop, is_transpose=True)

        nc.vector.tensor_tensor(gap_rows[0:2, 0:2, :], bias_rows[0:2, 0:2, :], bias_rows[0:2, 2:3, :].to_broadcast([2, 2, P]), ALU.subtract)
        gap01_row = sb.tile([P, P], F32, name="gap01_row", align_bytes=64)
        nc.vector.tensor_tensor(gap01_row[0:2, :], bias_rows[0:2, 0, :], bias_rows[0:2, 1, :], ALU.subtract)
        nc.vector.tensor_scalar(gap_rows[0:2, 2, :], gap01_row[0:2, :], 0.5, None, ALU.mult)
        gaps_t = psum.tile([P, D, P], F32, name="gaps_t", tag="k12_t")
        for j in range(D):
            turn(gaps_t[:, j, :], gap_rows[:, j, :], True, True)
        gaps = sb.tile([P, D, 2], F32, name="gaps", align_bytes=64)
        nc.scalar.copy(gaps[:], gaps_t[:, :, 0:2])

        picked_scales = sb.tile([P, S], U8, name="picked_scales", align_bytes=64)
        picked_words = [sb.tile([P, S], U32, name="picked_words_0", align_bytes=64)]
        pieces = [slice(0, HALF), slice(HALF, HALF + P), slice(HALF + P, S)]
        parts = [slice(c * P, (c + 1) * P) for c in range(2)]

        w1_bf = [sb.tile([P, PACK * N], BF16, name="w1_bf16_%d" % g, align_bytes=64) for g in range(PASSES)]
        for g in range(PASSES):
            round_pass(nc.scalar.copy, w1_bf[g][:], w1_raw[g][:])
        nc.vector.tensor_copy(picked_words[0][:], words0[:].indirect(offs_t[:]))
        nc.vector.tensor_copy(picked_scales[:], x_planes[:].indirect(offs_t[:]))
        w1_q = quantize_weight(w1_bf[0], "w1a") + quantize_weight(w1_bf[1], "w1b", "w1b_codes")
        picked_words.append(sb.tile([P, S], U32, name="picked_words_1", tag="w1_raw_1", align_bytes=64))
        for cols in pieces:
            nc.vector.tensor_copy(picked_words[1][:, cols], words1[:].indirect(offs_t[:, cols.start // 16 : cols.stop // 16]))
        w2_bf = [sb.tile([P, PACK * N], BF16, name="w2_bf16_%d" % g, align_bytes=64) for g in range(PASSES)]
        w3_bf = [sb.tile([P, PACK * N], BF16, name="w3_bf16_%d" % g, align_bytes=64) for g in range(PASSES)]
        round_pass(nc.scalar.copy, w3_bf[0][:], w3_raw[0][:])
        round_pass(nc.scalar.copy, w3_bf[1][:], w3_raw[1][:], slice(0, 3 * N // 16))
        round_pass(nc.vector.tensor_copy, w3_bf[1][:], w3_raw[1][:], slice(3 * N // 16, N // 4))
        w3_q = quantize_weight(w3_bf[0], "w3a")
        round_pass(nc.vector.tensor_copy, w2_bf[0][:], w2_raw[0][:])
        w3_q = w3_q + quantize_weight(w3_bf[1], "w3b")
        w2_q = quantize_weight(w2_bf[0], "w2a")
        round_pass(nc.vector.tensor_copy, w2_bf[1][:], w2_raw[1][:], slice(N // 8, N // 4))

        kk = sb.tile([P, S], F32, name="kk", tag="w3_raw_1", align_bytes=64)
        kk_acc = [psum.tile([P, cols.stop - cols.start], F32, name="kk_acc_%d" % h, tag="kk_acc_%d" % h) for h, cols in enumerate(pieces)]
        for h, cols in enumerate(pieces):
            product_pass(kk_acc[h], w1_q, 0, cols)
        for h, cols in enumerate(pieces):
            product_pass(kk_acc[h], w1_q, 1, cols)
        for h, cols in enumerate(pieces):
            nc.scalar.copy(kk[:, cols], kk_acc[h][:])
        gate_acc = psum.tile([P, S], F32, name="gate_acc", tag="gate_acc")
        for g in range(PASSES):
            product_pass(gate_acc, w3_q, g, slice(0, S))

        def slice_of(offsets, c):
            return offsets[:, c * P // 16 : (c + 1) * P // 16]

        round_pass(nc.scalar.copy, w2_bf[1][:], w2_raw[1][:], slice(0, N // 8))
        minus_k2 = values("minus_k2")
        nc.scalar.activation(minus_k2[:], kk[:].indirect(p2[:]), ACT.Copy, scale=-1.0)
        gate_tanh = sb.tile([P, S], F32, name="gate_tanh", align_bytes=64)
        nc.scalar.activation(gate_tanh[:], gate_acc[:], ACT.Tanh, scale=0.5)
        k1 = [sb.tile([P, P], F32, name="k1_0", align_bytes=64), reuse.tile([P, P], F32, name="k1_1", offset=1280, align_bytes=64)]
        nc.vector.tensor_copy(k1[0][:], kk[:].indirect(slice_of(p1, 0)))
        w2_q = w2_q + quantize_weight(w2_bf[1], "w2b", "w2b_codes")
        nc.vector.tensor_copy(k1[1][:], kk[:].indirect(slice_of(p1, 1)))
        k01 = reuse.tile([P, V], F32, name="k01", offset=256, align_bytes=64)
        for c in range(2):
            nc.vector.tensor_tensor(k01[:, parts[c]], kk[:].indirect(slice_of(p0, c)), k1[c][:], ALU.subtract)

        k12_t = psum.tile([P, V], F32, name="k12_t", tag="k12_t")
        k01_t = [psum.tile([P, P], F32, name="k01_t_%d" % c, tag=("kk_acc_2", "k01_t")[c]) for c in range(2)]
        k02_t = [psum.tile([P, P], F32, name="k02_t_%d" % c, tag="kk_acc_%d" % c) for c in range(2)]
        e12_t, e02_t, t01_t = values("e12_t"), values("e02_t"), values("t01_t")
        shares = [slice(0, HALF), slice(HALF, S)]
        vv_acc = [psum.tile([P, HALF], F32, name="vv_acc_%d" % h, tag="vv_acc_%d" % h) for h in range(2)]
        for g in range(PASSES):
            for h in range(2):
                product_pass(vv_acc[h], w2_q, g, shares[h])
        vv = sb.tile([P, S], F32, name="vv", align_bytes=64)
        for h in range(2):
            nc.scalar.copy(vv[:, shares[h]], vv_acc[h][:])
        own_tanh = sb.tile([P, V], F32, name="own_tanh", tag="w2b_codes", align_bytes=64)
        nc.vector.tensor_copy(own_tanh[:, parts[0]], gate_tanh[:].indirect(slice_of(own_t, 0)))
        nc.scalar.activation(own_tanh[:, parts[1]], gate_tanh[:].indirect(slice_of(own_t, 1)), ACT.Copy)
        for c in (1, 0):
            turn(k12_t[:, parts[c]], k1[c][:], True, False)
            turn(k12_t[:, parts[c]], minus_k2[:, parts[c]], False, True)
        for c in range(2):
            nc.scalar.activation(e12_t[:, parts[c]], k12_t[:, parts[c]], ACT.Exp, bias=gaps[:, 1, c : c + 1])
        for c in range(2):
            turn(k01_t[c][:], k01[:, parts[c]], True, True)
        for c in range(2):
            turn(k02_t[c][:], k01[:, parts[c]], True, False)
            turn(k02_t[c][:], k1[c][:], False, False)
            turn(k02_t[c][:], minus_k2[:, parts[c]], False, True)
        for c in range(2):
            nc.scalar.activation(t01_t[:, parts[c]], k01_t[c][:], ACT.Tanh, bias=gaps[:, 2, c : c + 1], scale=0.5)
        for c in range(2):
            nc.scalar.activation(e02_t[:, parts[c]], k02_t[c][:], ACT.Exp, bias=gaps[:, 0, c : c + 1])
        t01 = psum.tile([P, V], F32, name="t01", tag="k12_t")
        for c in parts:
            turn(t01[:, c], t01_t[:, c], True, True)
        e_sum = psum.tile([P, V], F32, name="e_sum", tag="gate_acc")
        root, half_w2 = values("root"), values("half_w2")
        for c in parts:
            turn(e_sum[:, c], e12_t[:, c], True, False)
            turn(e_sum[:, c], e02_t[:, c], False, True)
        for c in parts:
            nc.scalar.activation(root[:, c], e_sum[:, c], ACT.Abs_reciprocal_sqrt, bias=2.0, scale=2.0)
        for c in parts:
            nc.scalar.activation(half_w2[:, c], root[:, c], ACT.Square)

        v1, dv = values("v1"), values("dv")
        step, mean, rest, pull, result = values("step"), values("mean"), values("rest"), values("pull"), values("result")
        gated_mean, gated_rest = values("gated_mean"), values("gated_rest")
        for c in range(2):
            nc.vector.tensor_copy(v1[:, parts[c]], vv[:].indirect(slice_of(p1, c)))
        for c in range(2):
            nc.vector.tensor_tensor(dv[:, parts[c]], vv[:].indirect(slice_of(p0, c)), v1[:, parts[c]], ALU.subtract)
        for c in parts:
            nc.vector.scalar_tensor_tensor(step[:, c], t01[:, c], 1.0, dv[:, c], ALU.add, ALU.mult)
        for c in parts:
            nc.vector.scalar_tensor_tensor(mean[:, c], step[:, c], 0.5, v1[:, c], ALU.mult, ALU.add)
        for c in range(2):
            nc.vector.tensor_tensor(rest[:, parts[c]], vv[:].indirect(slice_of(p2, c)), mean[:, parts[c]], ALU.subtract)
        nc.vector.scalar_tensor_tensor(gated_mean[:], own_tanh[:], 1.0, mean[:], ALU.add, ALU.mult)
        for c in parts:
            nc.vector.scalar_tensor_tensor(gated_rest[:, c], own_tanh[:, c], 1.0, rest[:, c], ALU.add, ALU.mult)
        for c in parts:
            nc.vector.tensor_tensor(pull[:, c], gated_rest[:, c], half_w2[:, c], ALU.mult)
        for c in parts:
            nc.vector.scalar_tensor_tensor(result[:, c], gated_mean[:, c], 0.5, pull[:, c], ALU.mult, ALU.add)
            nc.sync.dma_start(out[:, c], result[:, c])
